import numpy as np
import ml_dtypes


def mxq(x, axis, fmt="e4m3"):
    dtype, down = {"e4m3": (ml_dtypes.float8_e4m3fn, 7), "e5m2": (ml_dtypes.float8_e5m2, 14)}[fmt]
    v = np.moveaxis(np.asarray(x, np.float32).astype(ml_dtypes.bfloat16).astype(np.float64), axis, -1)
    blocks = v.reshape(v.shape[:-1] + (-1, 32))
    amax = np.abs(blocks).max(-1, keepdims=True)
    byte = np.maximum(np.where(amax > 0, np.frexp(amax)[1] - 1 + 127, 0) - down, 1)
    scale = np.exp2(byte - 127.0)
    codes = (blocks / scale).astype(np.float32).astype(dtype).astype(np.float64)
    return np.moveaxis((codes * scale).reshape(v.shape), -1, axis)


WIDE = False


def mx_kscale(k):
    if not WIDE:
        return np.ones(k)
    levels = np.array([10, -10, 5, -5, 0])
    if k % 512:
        return np.exp2(np.random.permutation(np.resize(levels, k // 32))).repeat(32)
    a = np.empty((k // 512, 16))
    for p in range(k // 512):
        a[p, :8] = np.random.permutation(np.resize(levels, 8))
        for g in range(8):
            far = levels[np.abs(levels - a[p, g]) >= 10]
            a[p, g + 8] = far[np.random.randint(len(far))]
    return np.exp2(a.ravel()).repeat(32)


def f64(x):
    return np.asarray(x).astype(np.float64)


def striped(idx):
    return np.tile(np.asarray(idx).reshape(-1, 16).T, (8, 1)).astype(np.uint16)


def unstriped(offs):
    return offs[:16].T.reshape(-1).astype(np.int64)


E2M1 = np.array([0.0, 0.5, 1.0, 1.5, 2.0, 3.0, 4.0, 6.0, -0.0, -0.5, -1.0, -1.5, -2.0, -3.0, -4.0, -6.0])


def pack_weight(w, fmt):
    k, n = w.shape
    w = f64(np.asarray(w, np.float32).astype(ml_dtypes.bfloat16)).reshape(k // 32, 32, n)
    amax = np.abs(w).max(1)
    if fmt == "e4m3":
        byte = np.frexp(amax)[1] - 1 + 127 - 7
    else:
        mant, ex = np.frexp(amax / 6.0)
        byte = np.where(mant > 0.5, ex, ex - 1) + 127
    byte = np.clip(np.where(amax > 0, byte, 1), 1, 254)
    scaled = (w * np.exp2(127.0 - byte)[:, None, :]).reshape(k, n).astype(np.float32)
    by_word = np.ascontiguousarray(scaled.reshape(k // 512, 128, 4, n).transpose(0, 1, 3, 2))
    if fmt == "e4m3":
        words = by_word.astype(ml_dtypes.float8_e4m3fn).view(np.uint8)
    else:
        c = by_word.astype(ml_dtypes.float4_e2m1fn).view(np.uint8) & 0xF
        words = (c[..., 0::2] | (c[..., 1::2] << 4)).reshape(k // 512, 128, 2 * n)
    return np.ascontiguousarray(words), np.ascontiguousarray(byte.astype(np.uint8).reshape(k // 512, 16, n))


def unpack_weight(words, scales, fmt):
    g, _, n = scales.shape
    words = np.ascontiguousarray(words).reshape(g, 128, n, -1)
    if fmt == "e4m3":
        vals = words.view(ml_dtypes.float8_e4m3fn).astype(np.float64)
    else:
        nib = np.empty((g, 128, n, 4), np.uint8)
        nib[..., 0::2] = words & 0xF
        nib[..., 1::2] = words >> 4
        vals = E2M1[nib]
    vals = vals * np.repeat(np.exp2(scales.astype(np.float64) - 127.0), 8, axis=1)[..., None]
    return vals.transpose(0, 1, 3, 2).reshape(g * 512, n)


D, T, U, I, J, G = 512, 1024, 1024, 256, 512, 64


def setup_inputs():
    n = np.random.standard_normal
    idx = np.random.permutation(T)[:I]
    idx2 = np.random.permutation(U)[:J]
    fd = mx_kscale(D)
    fj = mx_kscale(J)
    tj = np.ones(U)
    tj[idx2] = fj
    tabbp = pack_weight(n((D, U)) / fd[:, None], "e2m1")
    return {
        "taba": (n((D, T)) * 1 / np.sqrt(D) * fd[:, None]).astype(np.float32),
        "tabb_words": tabbp[0],
        "tabb_scales": tabbp[1],
        "temper": (np.random.uniform(0.5, 2.0, (I, 1))).astype(np.float32),
        "gw": (n((I, G)) * 1.5).astype(np.float32),
        "js": (np.random.uniform(2.0, 8.0, (1, J)) * fj).astype(np.float32),
        "brows": (n((D, U)) / tj).astype(np.float32),
        "old": (n((D, T)) * 2.0).astype(np.float32),
        "fade": (np.random.uniform(0.5, 1.0, (1, T))).astype(np.float32),
        "offs": striped(idx),
        "offs2": striped(idx2),
    }


def reference(taba, tabb_words, tabb_scales, temper, gw, js, brows, old, fade, offs, offs2):
    idx = unstriped(offs)
    idx2 = unstriped(offs2)
    tabbu = unpack_weight(tabb_words, tabb_scales, "e2m1")
    tabaidxq = mxq(f64(taba)[:, idx], 0, "e4m3")
    tabbidx2g = tabbu[:, idx2]
    s = tabaidxq.T @ tabbidx2g
    p = np.exp(s * f64(temper))
    z = p.reshape(I, G, J // G).sum(axis=2)
    pl1 = np.log(z) / f64(temper)
    dpl1 = f64(gw) * (1.0 - np.square(np.tanh(pl1 - 2.0)))
    dz = dpl1 / f64(temper) / z
    r1 = np.repeat(dz, J // G, axis=1)
    ds = r1 * p * f64(temper)
    gs = ds * f64(js)
    gt1 = gs.T
    bt = f64(brows)[:, idx2].T
    btq = mxq(bt, 0, "e4m3")
    gt1q = mxq(gt1, 0, "e4m3")
    gx1 = btq.T @ gt1q
    gf = np.zeros((D, T))
    gf[:, idx] = gx1
    y = f64(old) * f64(fade) + gf
    return y

@@ -1,0 +1,241 @@
+from contextlib import ExitStack
+
+import concourse.mybir as mybir
+from concourse.masks import make_identity
+
+D, T, U, I, J, G = 512, 1024, 1024, 256, 512, 64
+FLOPS = 2 * 2 * D * I * J
+
+F32 = mybir.dt.float32
+BF16 = mybir.dt.bfloat16
+I32 = mybir.dt.int32
+U32 = mybir.dt.uint32
+U16 = mybir.dt.uint16
+U8 = mybir.dt.uint8
+FP8X4 = mybir.dt.float8_e4m3fn_x4
+FP4X4 = mybir.dt.float4_e2m1fn_x4
+ALU = mybir.AluOpType
+ACT = mybir.ActivationFunctionType
+AX = mybir.AxisListType
+
+P = 128
+PACK = 4
+MODES = ["G","G","X","X"]
+
+
+def tile_attend_blogpool_x_kernel(tc, taba, tabb_words, tabb_scales, temper, gw, js, brows, old, fade, offs, offs2, out):
+    nc = tc.nc
+    with ExitStack() as ctx:
+        lists = ctx.enter_context(tc.tile_pool(name="lists", bufs=1))
+        sb = ctx.enter_context(tc.tile_pool(name="sb", bufs=1))
+        ps = ctx.enter_context(tc.psum_pool(name="ps", bufs=1))
+
+        def bank(b, shape, name):
+            return ps.tile(shape, F32, name=name, tag="bank%d" % b)
+
+        idx = lists.tile([P, I // 16], U16, name="idx")
+        idx2 = lists.tile([P, J // 16], U16, name="idx2")
+
+        sc_all = sb.tile([P, U], U8, name="sc_all", align_bytes=64)
+        nc.vector.memset(sc_all[:].bitcast(I32), 0)
+        rows = sb.tile([P, P], F32, name="rows")
+        nc.vector.memset(rows[:], 0.0)
+        zero = sb.tile([P, 1], F32, name="zero")
+        nc.vector.memset(zero[:], 0.0)
+        ident = sb.tile([P, P], F32, name="ident")
+        make_identity(nc, ident[:])
+        win = [sb.tile([P, T], F32, name="win%d" % c) for c in range(4)]
+        for c in range(4):
+            nc.gpsimd.memset(win[c][:], 0.0)
+
+        ta = [sb.tile([P, T], F32, name="ta%d" % t) for t in range(PACK)]
+        ta_src = taba.rearrange("(p t) c -> p t c", t=PACK)
+        words_all = sb.tile([P, U], U16, name="words_all", align_bytes=64)
+        js_col = sb.tile([P, PACK], F32, name="js_col")
+        gw_sb = sb.tile([P, 2, G], F32, name="gw_sb")
+        nc.sync.dma_start(idx2[:], offs2)
+        nc.sync.dma_start(words_all[:].bitcast(I32), tabb_words[0].bitcast(I32))
+        for q in range(4):
+            nc.sync.dma_start(sc_all[32 * q : 32 * q + 4, :].bitcast(I32), tabb_scales[0, 4 * q : 4 * q + 4, :].bitcast(I32))
+        nc.sync.dma_start(idx[:], offs)
+        nc.sync.dma_start(ta[0][:], ta_src[:, 0, :])
+        nc.sync.dma_start(ta[1][:], ta_src[:, 1, :])
+        nc.sync.dma_start(rows[8:10, :], temper.rearrange("(h p) o -> h (p o)", p=P))
+        nc.sync.dma_start(rows[0:8, :], fade.rearrange("o (k p) -> (o k) p", p=P))
+        nc.sync.dma_start(ta[2][:], ta_src[:, 2, :])
+        nc.sync.dma_start(ta[3][:], ta_src[:, 3, :])
+
+        br = [sb.tile([P, U], F32, name="br%d" % c) for c in range(4)]
+        ol = [sb.tile([P, T], F32, name="ol%d" % c) for c in range(4)]
+        for kind, c in [["b",0],["o",0],["b",1],["o",1],["b",2],["b",3],["o",2],["o",3]]:
+            if kind == "b":
+                nc.sync.dma_start(br[c][:], brows[c * P : (c + 1) * P, :])
+                if c == 0:
+                    nc.sync.dma_start(gw_sb[:], gw.rearrange("(h p) g -> p h g", p=P))
+                    nc.sync.dma_start(js_col[:], js.rearrange("o (p t) -> p (o t)", t=PACK))
+            else:
+                nc.sync.dma_start(ol[c][:], old[c * P : (c + 1) * P, :])
+
+        warm = sb.tile([P, 1], F32, name="warm")
+        nc.scalar.activation(warm[:], zero[:], ACT.Exp)
+
+        rows_t = bank(0, [P, P], "rows_t")
+        nc.tensor.transpose(rows_t[:], rows[:], ident[:])
+        cols = sb.tile([P, 16], F32, name="cols")
+        nc.scalar.copy(cols[:], rows_t[:, 0:16])
+        fade_bc = sb.tile([P, T], F32, name="fade_bc")
+        if any(m != "X" for m in MODES):
+            for hf in range(2):
+                fb = bank(2 + hf, [P, 4, P], "fb%d" % hf)
+                for k in range(4):
+                    col = 4 * hf + k
+                    nc.tensor.transpose(fb[:, k, :], cols[:, col : col + 1].to_broadcast([P, P]), ident[:])
+                nc.scalar.copy(fade_bc[:, hf * 512 : (hf + 1) * 512], fb[:].rearrange("p k n -> p (k n)"))
+
+        a_in = sb.tile([P, I, PACK], BF16, name="a_in", align_bytes=64)
+        words_g = sb.tile([P, J], U16, name="words_g", align_bytes=64)
+        sc_g = sb.tile([P, J], U8, name="sc_g", align_bytes=64)
+        nc.vector.tensor_copy(words_g[:], words_all[:].indirect(idx2[:]))
+        nc.vector.tensor_copy(sc_g[:], sc_all[:].indirect(idx2[:]))
+        for t in range(3):
+            nc.vector.tensor_copy(a_in[:, :, t], ta[t][:].indirect(idx[:]))
+        inv_t = sb.tile([P, 2], F32, name="inv_t")
+        nc.vector.reciprocal(inv_t[:], cols[:, 8:10])
+        a_codes = sb.tile([P, I], U32, name="a_codes", align_bytes=64)
+        a_sc = sb.tile([P, I], U8, name="a_sc", align_bytes=64)
+        for h in range(2):
+            nc.vector.tensor_copy(a_in[:, h * P : (h + 1) * P, 3], ta[3][:].indirect(idx[:, 8 * h : 8 * h + 8]))
+        for h in range(2):
+            hs = slice(h * P, (h + 1) * P)
+            nc.vector.quantize_mx(out=a_codes[:, hs].bitcast(FP8X4), scales=a_sc[:, hs], in_=a_in[:, hs, :].rearrange("p i t -> p (i t)"))
+
+        p_sb = [sb.tile([P, J], F32, name="p%d" % h) for h in range(2)]
+        z = sb.tile([P, 2, G], F32, name="z")
+        for h in range(2):
+            hs = slice(h * P, (h + 1) * P)
+            s = bank(h, [P, J], "s%d" % h)
+            nc.tensor.matmul_mx(out=s[:], lhsT=a_codes[:, hs].bitcast(FP8X4), lhsT_scale=a_sc[:, hs],
+                                rhs=words_g[:].bitcast(FP4X4), rhs_scale=sc_g[:], start=True, stop=True)
+            nc.scalar.activation(p_sb[h][:], s[:], ACT.Exp, scale=cols[:, 8 + h : 9 + h])
+
+        bg = [sb.tile([P, J], BF16, name="bg%d" % c, align_bytes=64) for c in range(4)]
+        bt_in = [sb.tile([P, P, PACK], BF16, name="bt_in%d" % c, align_bytes=64) for c in range(4)]
+        bt_codes = [sb.tile([P, P], U32, name="bt_codes%d" % c, align_bytes=64) for c in range(4)]
+        bt_sc = [sb.tile([P, P], U8, name="bt_sc%d" % c, align_bytes=64) for c in range(4)]
+        bt_ps = {}
+
+        def gather_b(c):
+            nc.vector.tensor_copy(bg[c][:], br[c][:].indirect(idx2[:]))
+
+        def turn_b(c):
+            bt_ps[c] = bank(4 + c % 2, [P, 2, P], "btp%d" % c)
+            w = bg[c][:].bitcast(F32)
+            for u in range(2):
+                nc.tensor.transpose(bt_ps[c][:, u, :], w[:, u : J // 2 : 2], ident[:])
+
+        def copy_b(c):
+            nc.scalar.copy(bt_in[c][:].rearrange("p d t -> p (d t)").bitcast(F32).rearrange("p (d u) -> p d u", u=2),
+                           bt_ps[c][:].rearrange("p u d -> p d u"))
+
+        def quant_b(c):
+            nc.vector.quantize_mx(out=bt_codes[c][:].bitcast(FP8X4), scales=bt_sc[c][:], in_=bt_in[c][:].rearrange("p d t -> p (d t)"))
+
+        gather_b(0)
+        for h in range(2):
+            nc.vector.tensor_reduce(z[:, h, :], p_sb[h][:].rearrange("p (g k) -> p g k", k=8), AX.X, ALU.add)
+        lz = sb.tile([P, 2, G], F32, name="lz")
+        nc.scalar.activation(lz[:], z[:], ACT.Ln)
+        inv_z = sb.tile([P, 2, G], F32, name="inv_z")
+        nc.scalar.activation(inv_z[:], lz[:], ACT.Exp, scale=-1.0)
+        th = sb.tile([P, 2, G], F32, name="th")
+        for h in range(2):
+            nc.scalar.activation(th[:, h, :], lz[:, h, :], ACT.Tanh, scale=inv_t[:, h : h + 1], bias=-2.0)
+        sq = sb.tile([P, 2 * G], F32, name="sq")
+        nc.scalar.activation(sq[:], th[:].rearrange("p h g -> p (h g)"), ACT.Square)
+
+        pt = [bank(2 + b, [P, 2, I], "pt%d" % b) for b in range(2)]
+        for t in range(PACK):
+            for h in range(2):
+                nc.tensor.transpose(pt[t // 2][:, t % 2, h * P : (h + 1) * P], p_sb[h][:, t:J:PACK], ident[:])
+        turn_b(0)
+
+        for c in range(4):
+            if MODES[c] == "G":
+                nc.gpsimd.tensor_tensor(ol[c][:], ol[c][:], fade_bc[:], ALU.mult)
+        for c in range(1, 4):
+            gather_b(c)
+        turn_b(1)
+
+        pj = sb.tile([P, PACK, I], F32, name="pj")
+        for t in range(PACK):
+            nc.scalar.activation(pj[:, t, :], pt[t // 2][:, t % 2, :], ACT.Copy, scale=js_col[:, t : t + 1])
+
+        ge = sb.tile([P, 2 * G], F32, name="ge")
+        nc.vector.scalar_tensor_tensor(ge[:], inv_z[:].rearrange("p h g -> p (h g)"), -1.0, gw_sb[:].rearrange("p h g -> p (h g)"), ALU.mult, ALU.mult)
+        rd = sb.tile([P, 2 * G, 2], F32, name="rd")
+        nc.vector.scalar_tensor_tensor(rd[:], sq[:].unsqueeze(2).to_broadcast([P, 2 * G, 2]), 1.0,
+                                       ge[:].unsqueeze(2).to_broadcast([P, 2 * G, 2]), ALU.subtract, ALU.mult)
+        rt = bank(0, [P, I], "rt")
+        for h in range(2):
+            nc.tensor.transpose(rt[:, h * P : (h + 1) * P], rd[:, h * G : (h + 1) * G, :].rearrange("p g e -> p (g e)"), ident[:])
+        for c in range(2):
+            copy_b(c)
+            turn_b(c + 2)
+        g_in = sb.tile([P, I, PACK], BF16, name="g_in", align_bytes=64)
+        nc.vector.tensor_tensor(g_in[:], pj[:].rearrange("p t i -> p i t"), rt[:].unsqueeze(2).to_broadcast([P, I, PACK]), ALU.mult)
+        quant_b(0)
+        g_codes = sb.tile([P, I], U32, name="g_codes", align_bytes=64)
+        g_sc = sb.tile([P, I], U8, name="g_sc", align_bytes=64)
+        nc.vector.quantize_mx(out=g_codes[:].bitcast(FP8X4), scales=g_sc[:], in_=g_in[:].rearrange("p i t -> p (i t)"))
+        quant_b(1)
+        for c in range(2, 4):
+            copy_b(c)
+            quant_b(c)
+        for c in range(4):
+            if MODES[c] == "V":
+                nc.vector.tensor_tensor(ol[c][:], ol[c][:], fade_bc[:], ALU.mult)
+
+        gx_sb = [sb.tile([P, I], F32, name="gx%d" % c) for c in range(4)]
+        for c in range(4):
+            gx = bank(2 + c % 2, [P, I], "gxp%d" % c)
+            nc.tensor.matmul_mx(out=gx[:], lhsT=bt_codes[c][:].bitcast(FP8X4), lhsT_scale=bt_sc[c][:],
+                                rhs=g_codes[:].bitcast(FP8X4), rhs_scale=g_sc[:], start=True, stop=True)
+            nc.scalar.copy(gx_sb[c][:], gx[:])
+
+        xs = [c for c in range(4) if MODES[c] == "X"]
+        back = {}
+        free_banks = [0, 1, 4, 5]
+        for x0 in range(0, len(xs), 2):
+            pair = xs[x0 : x0 + 2]
+            n = len(pair)
+            oft = sb.tile([P, 8, n, P], F32, name="oft%d" % x0)
+            for kk in range(4):
+                ot = bank(6 + kk % 2, [P, 2, n, P], "ot%d_%d" % (x0, kk))
+                for e in range(2):
+                    k = 2 * kk + e
+                    for m, c in enumerate(pair):
+                        nc.tensor.transpose(ot[:, e, m, :], ol[c][:, k * P : (k + 1) * P], ident[:])
+                for e in range(2):
+                    k = 2 * kk + e
+                    nc.scalar.activation(oft[:, k, :, :], ot[:, e, :, :], ACT.Copy, scale=cols[:, k : k + 1])
+            for m, c in enumerate(pair):
+                for hf in range(2):
+                    back[(c, hf)] = bank(free_banks[2 * m + hf], [P, 4, P], "back%d_%d" % (c, hf))
+                    for e in range(4):
+                        nc.tensor.transpose(back[(c, hf)][:, e, :], oft[:, 4 * hf + e, m, :], ident[:])
+
+        for c in range(4):
+            nc.vector.tensor_copy(win[c][:].indirect(idx[:]), gx_sb[c][:])
+            rows_c = slice(c * P, (c + 1) * P)
+            if MODES[c] == "G":
+                nc.gpsimd.tensor_tensor(ol[c][:], ol[c][:], win[c][:], ALU.add)
+                nc.sync.dma_start(out[rows_c, :], ol[c][:])
+            else:
+                for hf in range(2):
+                    cs = slice(hf * 512, (hf + 1) * 512)
+                    res = sb.tile([P, 512], F32, name="res%d_%d" % (c, hf))
+                    if MODES[c] == "X":
+                        nc.vector.tensor_tensor(res[:], back[(c, hf)][:].rearrange("p e n -> p (e n)"), win[c][:, cs], ALU.add)
+                    else:
+                        nc.vector.tensor_tensor(res[:], ol[c][:, cs], win[c][:, cs], ALU.add)
+                    nc.sync.dma_start(out[rows_c, cs], res[:])

@@ -20,7 +20,7 @@ AX = mybir.AxisListType
 
 P = 128
 PACK = 4
-MODES = ["G","G","X","X"]
+MODES = ["X","X","X","X"]
 
 
 def tile_attend_blogpool_x_kernel(tc, taba, tabb_words, tabb_scales, temper, gw, js, brows, old, fade, offs, offs2, out):
@@ -44,9 +44,14 @@ def tile_attend_blogpool_x_kernel(tc, taba, tabb_words, tabb_scales, temper, gw,
         nc.vector.memset(zero[:], 0.0)
         ident = sb.tile([P, P], F32, name="ident")
         make_identity(nc, ident[:])
-        win = [sb.tile([P, T], F32, name="win%d" % c) for c in range(4)]
-        for c in range(4):
-            nc.gpsimd.memset(win[c][:], 0.0)
+        win = {}
+
+        def zero_window(c, tag):
+            win[c] = sb.tile([P, T], F32, name="win%d" % c, tag=tag)
+            nc.vector.memset(win[c][:].bitcast(I32), 0)
+
+        zero_window(0, "win0")
+        zero_window(1, "win1")
 
         ta = [sb.tile([P, T], F32, name="ta%d" % t) for t in range(PACK)]
         ta_src = taba.rearrange("(p t) c -> p t c", t=PACK)
@@ -65,9 +70,9 @@ def tile_attend_blogpool_x_kernel(tc, taba, tabb_words, tabb_scales, temper, gw,
         nc.sync.dma_start(ta[2][:], ta_src[:, 2, :])
         nc.sync.dma_start(ta[3][:], ta_src[:, 3, :])
 
-        br = [sb.tile([P, U], F32, name="br%d" % c) for c in range(4)]
+        br = [sb.tile([P, U], F32, name="br%d" % c, tag="br%d" % c) for c in range(4)]
         ol = [sb.tile([P, T], F32, name="ol%d" % c) for c in range(4)]
-        for kind, c in [["b",0],["o",0],["b",1],["o",1],["b",2],["b",3],["o",2],["o",3]]:
+        for kind, c in [["b",0],["b",1],["b",2],["b",3],["o",0],["o",1],["o",2],["o",3]]:
             if kind == "b":
                 nc.sync.dma_start(br[c][:], brows[c * P : (c + 1) * P, :])
                 if c == 0:
@@ -119,7 +124,7 @@ def tile_attend_blogpool_x_kernel(tc, taba, tabb_words, tabb_scales, temper, gw,
             nc.scalar.activation(p_sb[h][:], s[:], ACT.Exp, scale=cols[:, 8 + h : 9 + h])
 
         bg = [sb.tile([P, J], BF16, name="bg%d" % c, align_bytes=64) for c in range(4)]
-        bt_in = [sb.tile([P, P, PACK], BF16, name="bt_in%d" % c, align_bytes=64) for c in range(4)]
+        bt_in = {}
         bt_codes = [sb.tile([P, P], U32, name="bt_codes%d" % c, align_bytes=64) for c in range(4)]
         bt_sc = [sb.tile([P, P], U8, name="bt_sc%d" % c, align_bytes=64) for c in range(4)]
         bt_ps = {}
@@ -134,6 +139,7 @@ def tile_attend_blogpool_x_kernel(tc, taba, tabb_words, tabb_scales, temper, gw,
                 nc.tensor.transpose(bt_ps[c][:, u, :], w[:, u : J // 2 : 2], ident[:])
 
         def copy_b(c):
+            bt_in[c] = sb.tile([P, P, PACK], BF16, name="bt_in%d" % c, tag="late%d" % c, align_bytes=64)
             nc.scalar.copy(bt_in[c][:].rearrange("p d t -> p (d t)").bitcast(F32).rearrange("p (d u) -> p d u", u=2),
                            bt_ps[c][:].rearrange("p u d -> p d u"))
 
@@ -143,11 +149,12 @@ def tile_attend_blogpool_x_kernel(tc, taba, tabb_words, tabb_scales, temper, gw,
         gather_b(0)
         for h in range(2):
             nc.vector.tensor_reduce(z[:, h, :], p_sb[h][:].rearrange("p (g k) -> p g k", k=8), AX.X, ALU.add)
-        lz = sb.tile([P, 2, G], F32, name="lz")
-        nc.scalar.activation(lz[:], z[:], ACT.Ln)
+        lz = sb.tile([P, 2, G], F32, name="lz", tag="late0", align_bytes=64)
+        for h in range(2):
+            nc.scalar.activation(lz[:, h, :], z[:, h, :], ACT.Ln)
         inv_z = sb.tile([P, 2, G], F32, name="inv_z")
         nc.scalar.activation(inv_z[:], lz[:], ACT.Exp, scale=-1.0)
-        th = sb.tile([P, 2, G], F32, name="th")
+        th = sb.tile([P, 2, G], F32, name="th", tag="late1", align_bytes=64)
         for h in range(2):
             nc.scalar.activation(th[:, h, :], lz[:, h, :], ACT.Tanh, scale=inv_t[:, h : h + 1], bias=-2.0)
         sq = sb.tile([P, 2 * G], F32, name="sq")
@@ -166,7 +173,7 @@ def tile_attend_blogpool_x_kernel(tc, taba, tabb_words, tabb_scales, temper, gw,
             gather_b(c)
         turn_b(1)
 
-        pj = sb.tile([P, PACK, I], F32, name="pj")
+        pj = sb.tile([P, PACK, I], F32, name="pj", tag="pj")
         for t in range(PACK):
             nc.scalar.activation(pj[:, t, :], pt[t // 2][:, t % 2, :], ACT.Copy, scale=js_col[:, t : t + 1])
 
@@ -202,29 +209,35 @@ def tile_attend_blogpool_x_kernel(tc, taba, tabb_words, tabb_scales, temper, gw,
                                 rhs=g_codes[:].bitcast(FP8X4), rhs_scale=g_sc[:], start=True, stop=True)
             nc.scalar.copy(gx_sb[c][:], gx[:])
 
-        xs = [c for c in range(4) if MODES[c] == "X"]
         back = {}
-        free_banks = [0, 1, 4, 5]
-        for x0 in range(0, len(xs), 2):
-            pair = xs[x0 : x0 + 2]
-            n = len(pair)
-            oft = sb.tile([P, 8, n, P], F32, name="oft%d" % x0)
-            for kk in range(4):
-                ot = bank(6 + kk % 2, [P, 2, n, P], "ot%d_%d" % (x0, kk))
-                for e in range(2):
-                    k = 2 * kk + e
-                    for m, c in enumerate(pair):
-                        nc.tensor.transpose(ot[:, e, m, :], ol[c][:, k * P : (k + 1) * P], ident[:])
-                for e in range(2):
-                    k = 2 * kk + e
-                    nc.scalar.activation(oft[:, k, :, :], ot[:, e, :, :], ACT.Copy, scale=cols[:, k : k + 1])
-            for m, c in enumerate(pair):
-                for hf in range(2):
-                    back[(c, hf)] = bank(free_banks[2 * m + hf], [P, 4, P], "back%d_%d" % (c, hf))
-                    for e in range(4):
-                        nc.tensor.transpose(back[(c, hf)][:, e, :], oft[:, 4 * hf + e, m, :], ident[:])
+        oft = {}
 
+        def fade_pair(c0):
+            oft[c0] = sb.tile([P, 8, 2, P], F32, name="oft%d" % c0)
+            for kk in range(4):
+                ot = bank(6 + kk % 2, [P, 2, 2, P], "ot%d_%d" % (c0, kk))
+                for e in range(2):
+                    k = 2 * kk + e
+                    for m in range(2):
+                        nc.tensor.transpose(ot[:, e, m, :], ol[c0 + m][:, k * P : (k + 1) * P], ident[:])
+                for e in range(2):
+                    k = 2 * kk + e
+                    nc.scalar.activation(oft[c0][:, k, :, :], ot[:, e, :, :], ACT.Copy, scale=cols[:, k : k + 1])
+
+        def turn_back(c):
+            for hf in range(2):
+                back[(c, hf)] = bank((0, 1, 4, 5)[2 * (c % 2) + hf], [P, 4, P], "back%d_%d" % (c, hf))
+                for e in range(4):
+                    nc.tensor.transpose(back[(c, hf)][:, e, :], oft[c - c % 2][:, 4 * hf + e, c % 2, :], ident[:])
+
+        for c0 in (0, 2):
+            if MODES[c0] == "X":
+                fade_pair(c0)
+
+        win[2], win[3] = win[0], win[1]
         for c in range(4):
+            if MODES[c] == "X":
+                turn_back(c)
             nc.vector.tensor_copy(win[c][:].indirect(idx[:]), gx_sb[c][:])
             rows_c = slice(c * P, (c + 1) * P)
             if MODES[c] == "G":

@@ -20,7 +20,7 @@ AX = mybir.AxisListType
 
 P = 128
 PACK = 4
-MODES = ["X","X","X","X"]
+MODES = ["G","G","W","X"]
 
 
 def tile_attend_blogpool_x_kernel(tc, taba, tabb_words, tabb_scales, temper, gw, js, brows, old, fade, offs, offs2, out):
@@ -37,7 +37,7 @@ def tile_attend_blogpool_x_kernel(tc, taba, tabb_words, tabb_scales, temper, gw,
         idx2 = lists.tile([P, J // 16], U16, name="idx2")
 
         sc_all = sb.tile([P, U], U8, name="sc_all", align_bytes=64)
-        nc.vector.memset(sc_all[:].bitcast(I32), 0)
+        nc.gpsimd.memset(sc_all[:].bitcast(I32), 0)
         rows = sb.tile([P, P], F32, name="rows")
         nc.vector.memset(rows[:], 0.0)
         zero = sb.tile([P, 1], F32, name="zero")
@@ -48,10 +48,12 @@ def tile_attend_blogpool_x_kernel(tc, taba, tabb_words, tabb_scales, temper, gw,
 
         def zero_window(c, tag):
             win[c] = sb.tile([P, T], F32, name="win%d" % c, tag=tag)
-            nc.vector.memset(win[c][:].bitcast(I32), 0)
+            nc.gpsimd.memset(win[c][:].bitcast(I32), 0)
 
         zero_window(0, "win0")
         zero_window(1, "win1")
+        zero_window(2, "win2")
+        win[3] = win[0]
 
         ta = [sb.tile([P, T], F32, name="ta%d" % t) for t in range(PACK)]
         ta_src = taba.rearrange("(p t) c -> p t c", t=PACK)
@@ -61,18 +63,18 @@ def tile_attend_blogpool_x_kernel(tc, taba, tabb_words, tabb_scales, temper, gw,
         nc.sync.dma_start(idx2[:], offs2)
         nc.sync.dma_start(words_all[:].bitcast(I32), tabb_words[0].bitcast(I32))
         for q in range(4):
-            nc.sync.dma_start(sc_all[32 * q : 32 * q + 4, :].bitcast(I32), tabb_scales[0, 4 * q : 4 * q + 4, :].bitcast(I32))
-        nc.sync.dma_start(idx[:], offs)
+            nc.scalar.dma_start(sc_all[32 * q : 32 * q + 4, :].bitcast(I32), tabb_scales[0, 4 * q : 4 * q + 4, :].bitcast(I32))
         nc.sync.dma_start(ta[0][:], ta_src[:, 0, :])
+        nc.sync.dma_start(idx[:], offs)
         nc.sync.dma_start(ta[1][:], ta_src[:, 1, :])
         nc.sync.dma_start(rows[8:10, :], temper.rearrange("(h p) o -> h (p o)", p=P))
         nc.sync.dma_start(rows[0:8, :], fade.rearrange("o (k p) -> (o k) p", p=P))
         nc.sync.dma_start(ta[2][:], ta_src[:, 2, :])
         nc.sync.dma_start(ta[3][:], ta_src[:, 3, :])
 
-        br = [sb.tile([P, U], F32, name="br%d" % c, tag="br%d" % c) for c in range(4)]
+        br = [sb.tile([P, U], F32, name="br%d" % c, tag=("br0", "br1", "br2", "late4")[c], align_bytes=64) for c in range(4)]
         ol = [sb.tile([P, T], F32, name="ol%d" % c) for c in range(4)]
-        for kind, c in [["b",0],["b",1],["b",2],["b",3],["o",0],["o",1],["o",2],["o",3]]:
+        for kind, c in [["b",0],["o",0],["b",1],["b",2],["b",3],["o",1],["o",2],["o",3]]:
             if kind == "b":
                 nc.sync.dma_start(br[c][:], brows[c * P : (c + 1) * P, :])
                 if c == 0:
@@ -88,6 +90,8 @@ def tile_attend_blogpool_x_kernel(tc, taba, tabb_words, tabb_scales, temper, gw,
         nc.tensor.transpose(rows_t[:], rows[:], ident[:])
         cols = sb.tile([P, 16], F32, name="cols")
         nc.scalar.copy(cols[:], rows_t[:, 0:16])
+        t_last = sb.tile([P, 1], F32, name="t_last", tag="late0", align_bytes=64)
+        nc.scalar.copy(t_last[:], rows_t[:, 9:10])
         fade_bc = sb.tile([P, T], F32, name="fade_bc")
         if any(m != "X" for m in MODES):
             for hf in range(2):
@@ -114,32 +118,35 @@ def tile_attend_blogpool_x_kernel(tc, taba, tabb_words, tabb_scales, temper, gw,
             hs = slice(h * P, (h + 1) * P)
             nc.vector.quantize_mx(out=a_codes[:, hs].bitcast(FP8X4), scales=a_sc[:, hs], in_=a_in[:, hs, :].rearrange("p i t -> p (i t)"))
 
-        p_sb = [sb.tile([P, J], F32, name="p%d" % h) for h in range(2)]
-        z = sb.tile([P, 2, G], F32, name="z")
+        p_sb = [sb.tile([P, PACK, P], F32, name="p%d" % h, tag="p%d" % h, align_bytes=64) for h in range(2)]
+        z0 = sb.tile([P, G], F32, name="z0")
+        z1 = sb.tile([P, G], F32, name="z1", tag="late1", align_bytes=64)
+        z = [z0, z1]
         for h in range(2):
             hs = slice(h * P, (h + 1) * P)
             s = bank(h, [P, J], "s%d" % h)
             nc.tensor.matmul_mx(out=s[:], lhsT=a_codes[:, hs].bitcast(FP8X4), lhsT_scale=a_sc[:, hs],
                                 rhs=words_g[:].bitcast(FP4X4), rhs_scale=sc_g[:], start=True, stop=True)
-            nc.scalar.activation(p_sb[h][:], s[:], ACT.Exp, scale=cols[:, 8 + h : 9 + h])
+            nc.scalar.activation(p_sb[h][:], s[:].rearrange("p (m t) -> p t m", t=PACK), ACT.Exp, scale=(cols[:, 8:9], t_last[:])[h])
 
-        bg = [sb.tile([P, J], BF16, name="bg%d" % c, align_bytes=64) for c in range(4)]
+        bg = {}
         bt_in = {}
         bt_codes = [sb.tile([P, P], U32, name="bt_codes%d" % c, align_bytes=64) for c in range(4)]
         bt_sc = [sb.tile([P, P], U8, name="bt_sc%d" % c, align_bytes=64) for c in range(4)]
         bt_ps = {}
 
         def gather_b(c):
+            bg[c] = sb.tile([P, J], BF16, name="bg%d" % c, tag=("bg0", "p1", "bg2", "bg3")[c], align_bytes=64)
             nc.vector.tensor_copy(bg[c][:], br[c][:].indirect(idx2[:]))
 
         def turn_b(c):
-            bt_ps[c] = bank(4 + c % 2, [P, 2, P], "btp%d" % c)
+            bt_ps[c] = bank(4 + c, [P, 2, P], "btp%d" % c)
             w = bg[c][:].bitcast(F32)
             for u in range(2):
                 nc.tensor.transpose(bt_ps[c][:, u, :], w[:, u : J // 2 : 2], ident[:])
 
         def copy_b(c):
-            bt_in[c] = sb.tile([P, P, PACK], BF16, name="bt_in%d" % c, tag="late%d" % c, align_bytes=64)
+            bt_in[c] = sb.tile([P, P, PACK], BF16, name="bt_in%d" % c, tag="late%d" % (c + 2), align_bytes=64)
             nc.scalar.copy(bt_in[c][:].rearrange("p d t -> p (d t)").bitcast(F32).rearrange("p (d u) -> p d u", u=2),
                            bt_ps[c][:].rearrange("p u d -> p d u"))
 
@@ -148,63 +155,62 @@ def tile_attend_blogpool_x_kernel(tc, taba, tabb_words, tabb_scales, temper, gw,
 
         gather_b(0)
         for h in range(2):
-            nc.vector.tensor_reduce(z[:, h, :], p_sb[h][:].rearrange("p (g k) -> p g k", k=8), AX.X, ALU.add)
+            nc.vector.tensor_reduce(z[h][:], p_sb[h][:].rearrange("p t (g e) -> p g t e", e=2), AX.XY, ALU.add)
         lz = sb.tile([P, 2, G], F32, name="lz", tag="late0", align_bytes=64)
         for h in range(2):
-            nc.scalar.activation(lz[:, h, :], z[:, h, :], ACT.Ln)
-        inv_z = sb.tile([P, 2, G], F32, name="inv_z")
+            nc.scalar.activation(lz[:, h, :], z[h][:], ACT.Ln)
+        inv_z = sb.tile([P, 2, G], F32, name="inv_z", tag="late2", align_bytes=64)
         nc.scalar.activation(inv_z[:], lz[:], ACT.Exp, scale=-1.0)
         th = sb.tile([P, 2, G], F32, name="th", tag="late1", align_bytes=64)
         for h in range(2):
             nc.scalar.activation(th[:, h, :], lz[:, h, :], ACT.Tanh, scale=inv_t[:, h : h + 1], bias=-2.0)
-        sq = sb.tile([P, 2 * G], F32, name="sq")
+        sq = sb.tile([P, 2 * G], F32, name="sq", tag="late3", align_bytes=64)
         nc.scalar.activation(sq[:], th[:].rearrange("p h g -> p (h g)"), ACT.Square)
 
         pt = [bank(2 + b, [P, 2, I], "pt%d" % b) for b in range(2)]
         for t in range(PACK):
             for h in range(2):
-                nc.tensor.transpose(pt[t // 2][:, t % 2, h * P : (h + 1) * P], p_sb[h][:, t:J:PACK], ident[:])
+                nc.tensor.transpose(pt[t // 2][:, t % 2, h * P : (h + 1) * P], p_sb[h][:, t, :], ident[:])
         turn_b(0)
 
-        for c in range(4):
-            if MODES[c] == "G":
-                nc.gpsimd.tensor_tensor(ol[c][:], ol[c][:], fade_bc[:], ALU.mult)
+        of = {0: ol[0]}
+        nc.gpsimd.tensor_tensor(ol[0][:], ol[0][:], fade_bc[:], ALU.mult)
         for c in range(1, 4):
             gather_b(c)
-        turn_b(1)
+        for c in range(1, 4):
+            turn_b(c)
 
-        pj = sb.tile([P, PACK, I], F32, name="pj", tag="pj")
+        pj = sb.tile([P, PACK, I], F32, name="pj", tag="late1", align_bytes=64)
         for t in range(PACK):
             nc.scalar.activation(pj[:, t, :], pt[t // 2][:, t % 2, :], ACT.Copy, scale=js_col[:, t : t + 1])
 
-        ge = sb.tile([P, 2 * G], F32, name="ge")
+        ge = sb.tile([P, 2 * G], F32, name="ge", tag="late4", align_bytes=64)
         nc.vector.scalar_tensor_tensor(ge[:], inv_z[:].rearrange("p h g -> p (h g)"), -1.0, gw_sb[:].rearrange("p h g -> p (h g)"), ALU.mult, ALU.mult)
-        rd = sb.tile([P, 2 * G, 2], F32, name="rd")
+        rd = sb.tile([P, 2 * G, 2], F32, name="rd", tag="late5", align_bytes=64)
         nc.vector.scalar_tensor_tensor(rd[:], sq[:].unsqueeze(2).to_broadcast([P, 2 * G, 2]), 1.0,
                                        ge[:].unsqueeze(2).to_broadcast([P, 2 * G, 2]), ALU.subtract, ALU.mult)
         rt = bank(0, [P, I], "rt")
         for h in range(2):
             nc.tensor.transpose(rt[:, h * P : (h + 1) * P], rd[:, h * G : (h + 1) * G, :].rearrange("p g e -> p (g e)"), ident[:])
-        for c in range(2):
+        for c in range(4):
             copy_b(c)
-            turn_b(c + 2)
-        g_in = sb.tile([P, I, PACK], BF16, name="g_in", align_bytes=64)
+        g_in = sb.tile([P, I, PACK], BF16, name="g_in", tag="g_in", align_bytes=64)
         nc.vector.tensor_tensor(g_in[:], pj[:].rearrange("p t i -> p i t"), rt[:].unsqueeze(2).to_broadcast([P, I, PACK]), ALU.mult)
         quant_b(0)
         g_codes = sb.tile([P, I], U32, name="g_codes", align_bytes=64)
         g_sc = sb.tile([P, I], U8, name="g_sc", align_bytes=64)
         nc.vector.quantize_mx(out=g_codes[:].bitcast(FP8X4), scales=g_sc[:], in_=g_in[:].rearrange("p i t -> p (i t)"))
-        quant_b(1)
-        for c in range(2, 4):
-            copy_b(c)
+        for c in range(1, 4):
             quant_b(c)
         for c in range(4):
             if MODES[c] == "V":
                 nc.vector.tensor_tensor(ol[c][:], ol[c][:], fade_bc[:], ALU.mult)
 
+        of[1] = sb.tile([P, T], F32, name="of1", tag="late5", align_bytes=64)
+        nc.gpsimd.tensor_tensor(of[1][:], ol[1][:], fade_bc[:], ALU.mult)
         gx_sb = [sb.tile([P, I], F32, name="gx%d" % c) for c in range(4)]
         for c in range(4):
-            gx = bank(2 + c % 2, [P, I], "gxp%d" % c)
+            gx = bank((2, 3, 6, 7)[c], [P, I], "gxp%d" % c)
             nc.tensor.matmul_mx(out=gx[:], lhsT=bt_codes[c][:].bitcast(FP8X4), lhsT_scale=bt_sc[c][:],
                                 rhs=g_codes[:].bitcast(FP8X4), rhs_scale=g_sc[:], start=True, stop=True)
             nc.scalar.copy(gx_sb[c][:], gx[:])
@@ -215,7 +221,7 @@ def tile_attend_blogpool_x_kernel(tc, taba, tabb_words, tabb_scales, temper, gw,
         def fade_pair(c0):
             oft[c0] = sb.tile([P, 8, 2, P], F32, name="oft%d" % c0)
             for kk in range(4):
-                ot = bank(6 + kk % 2, [P, 2, 2, P], "ot%d_%d" % (c0, kk))
+                ot = bank(2 + kk % 2, [P, 2, 2, P], "ot%d_%d" % (c0, kk))
                 for e in range(2):
                     k = 2 * kk + e
                     for m in range(2):
@@ -231,24 +237,30 @@ def tile_attend_blogpool_x_kernel(tc, taba, tabb_words, tabb_scales, temper, gw,
                     nc.tensor.transpose(back[(c, hf)][:, e, :], oft[c - c % 2][:, 4 * hf + e, c % 2, :], ident[:])
 
         for c0 in (0, 2):
-            if MODES[c0] == "X":
+            if MODES[c0] in ("X", "W"):
                 fade_pair(c0)
-
-        win[2], win[3] = win[0], win[1]
+        faded = {}
         for c in range(4):
-            if MODES[c] == "X":
+            if MODES[c] in ("X", "W"):
                 turn_back(c)
+            if MODES[c] == "W":
+                for hf in range(1):
+                    faded[(c, hf)] = sb.tile([P, 512], F32, name="faded%d_%d" % (c, hf))
+                    nc.scalar.copy(faded[(c, hf)][:], back[(c, hf)][:].rearrange("p e n -> p (e n)"))
+
+        for c in range(4):
             nc.vector.tensor_copy(win[c][:].indirect(idx[:]), gx_sb[c][:])
             rows_c = slice(c * P, (c + 1) * P)
             if MODES[c] == "G":
-                nc.gpsimd.tensor_tensor(ol[c][:], ol[c][:], win[c][:], ALU.add)
-                nc.sync.dma_start(out[rows_c, :], ol[c][:])
+                full = sb.tile([P, T], F32, name="full%d" % c, tag="full%d" % c, align_bytes=64)
+                nc.gpsimd.tensor_tensor(full[:], of[c][:], win[c][:], ALU.add)
+                nc.sync.dma_start(out[rows_c, :], full[:])
             else:
                 for hf in range(2):
                     cs = slice(hf * 512, (hf + 1) * 512)
                     res = sb.tile([P, 512], F32, name="res%d_%d" % (c, hf))
-                    if MODES[c] == "X":
+                    if (c, hf) not in faded:
                         nc.vector.tensor_tensor(res[:], back[(c, hf)][:].rearrange("p e n -> p (e n)"), win[c][:, cs], ALU.add)
                     else:
-                        nc.vector.tensor_tensor(res[:], ol[c][:, cs], win[c][:, cs], ALU.add)
+                        nc.gpsimd.tensor_tensor(res[:], faded[(c, hf)][:], win[c][:, cs], ALU.add)
                     nc.sync.dma_start(out[rows_c, cs], res[:])

from contextlib import ExitStack

import concourse.mybir as mybir
from concourse.masks import make_identity

D, T, U, I, J, G = 512, 1024, 1024, 256, 512, 64
FLOPS = 2 * 2 * D * I * J

F32 = mybir.dt.float32
BF16 = mybir.dt.bfloat16
I32 = mybir.dt.int32
U32 = mybir.dt.uint32
U16 = mybir.dt.uint16
U8 = mybir.dt.uint8
FP8X4 = mybir.dt.float8_e4m3fn_x4
FP4X4 = mybir.dt.float4_e2m1fn_x4
ALU = mybir.AluOpType
ACT = mybir.ActivationFunctionType
AX = mybir.AxisListType

P = 128
PACK = 4
MODES = ["G","G","W","X"]


def tile_attend_blogpool_x_kernel(tc, taba, tabb_words, tabb_scales, temper, gw, js, brows, old, fade, offs, offs2, out):
    nc = tc.nc
    with ExitStack() as ctx:
        lists = ctx.enter_context(tc.tile_pool(name="lists", bufs=1))
        sb = ctx.enter_context(tc.tile_pool(name="sb", bufs=1))
        ps = ctx.enter_context(tc.psum_pool(name="ps", bufs=1))

        def bank(b, shape, name):
            return ps.tile(shape, F32, name=name, tag="bank%d" % b)

        idx = lists.tile([P, I // 16], U16, name="idx")
        idx2 = lists.tile([P, J // 16], U16, name="idx2")

        sc_all = sb.tile([P, U], U8, name="sc_all", align_bytes=64)
        nc.gpsimd.memset(sc_all[:].bitcast(I32), 0)
        rows = sb.tile([P, P], F32, name="rows")
        nc.vector.memset(rows[:], 0.0)
        zero = sb.tile([P, 1], F32, name="zero")
        nc.vector.memset(zero[:], 0.0)
        ident = sb.tile([P, P], F32, name="ident")
        make_identity(nc, ident[:])
        win = {}

        def zero_window(c, tag):
            win[c] = sb.tile([P, T], F32, name="win%d" % c, tag=tag)
            nc.gpsimd.memset(win[c][:].bitcast(I32), 0)

        zero_window(0, "win0")
        zero_window(1, "win1")
        zero_window(2, "win2")
        win[3] = win[0]

        ta = [sb.tile([P, T], F32, name="ta%d" % t) for t in range(PACK)]
        ta_src = taba.rearrange("(p t) c -> p t c", t=PACK)
        words_all = sb.tile([P, U], U16, name="words_all", align_bytes=64)
        js_col = sb.tile([P, PACK], F32, name="js_col")
        gw_sb = sb.tile([P, 2, G], F32, name="gw_sb")
        nc.sync.dma_start(idx2[:], offs2)
        nc.sync.dma_start(words_all[:].bitcast(I32), tabb_words[0].bitcast(I32))
        for q in range(4):
            nc.scalar.dma_start(sc_all[32 * q : 32 * q + 4, :].bitcast(I32), tabb_scales[0, 4 * q : 4 * q + 4, :].bitcast(I32))
        nc.sync.dma_start(ta[0][:], ta_src[:, 0, :])
        nc.sync.dma_start(idx[:], offs)
        nc.sync.dma_start(ta[1][:], ta_src[:, 1, :])
        nc.sync.dma_start(rows[8:10, :], temper.rearrange("(h p) o -> h (p o)", p=P))
        nc.sync.dma_start(rows[0:8, :], fade.rearrange("o (k p) -> (o k) p", p=P))
        nc.sync.dma_start(ta[2][:], ta_src[:, 2, :])
        nc.sync.dma_start(ta[3][:], ta_src[:, 3, :])

        br = [sb.tile([P, U], F32, name="br%d" % c, tag=("br0", "br1", "br2", "late4")[c], align_bytes=64) for c in range(4)]
        ol = [sb.tile([P, T], F32, name="ol%d" % c) for c in range(4)]
        for kind, c in [["b",0],["o",0],["b",1],["b",2],["b",3],["o",1],["o",2],["o",3]]:
            if kind == "b":
                nc.sync.dma_start(br[c][:], brows[c * P : (c + 1) * P, :])
                if c == 0:
                    nc.sync.dma_start(gw_sb[:], gw.rearrange("(h p) g -> p h g", p=P))
                    nc.sync.dma_start(js_col[:], js.rearrange("o (p t) -> p (o t)", t=PACK))
            else:
                nc.sync.dma_start(ol[c][:], old[c * P : (c + 1) * P, :])

        warm = sb.tile([P, 1], F32, name="warm")
        nc.scalar.activation(warm[:], zero[:], ACT.Exp)

        rows_t = bank(0, [P, P], "rows_t")
        nc.tensor.transpose(rows_t[:], rows[:], ident[:])
        cols = sb.tile([P, 16], F32, name="cols")
        nc.scalar.copy(cols[:], rows_t[:, 0:16])
        t_last = sb.tile([P, 1], F32, name="t_last", tag="late0", align_bytes=64)
        nc.scalar.copy(t_last[:], rows_t[:, 9:10])
        fade_bc = sb.tile([P, T], F32, name="fade_bc")
        if any(m != "X" for m in MODES):
            for hf in range(2):
                fb = bank(2 + hf, [P, 4, P], "fb%d" % hf)
                for k in range(4):
                    col = 4 * hf + k
                    nc.tensor.transpose(fb[:, k, :], cols[:, col : col + 1].to_broadcast([P, P]), ident[:])
                nc.scalar.copy(fade_bc[:, hf * 512 : (hf + 1) * 512], fb[:].rearrange("p k n -> p (k n)"))

        a_in = sb.tile([P, I, PACK], BF16, name="a_in", align_bytes=64)
        words_g = sb.tile([P, J], U16, name="words_g", align_bytes=64)
        sc_g = sb.tile([P, J], U8, name="sc_g", align_bytes=64)
        nc.vector.tensor_copy(words_g[:], words_all[:].indirect(idx2[:]))
        nc.vector.tensor_copy(sc_g[:], sc_all[:].indirect(idx2[:]))
        for t in range(3):
            nc.vector.tensor_copy(a_in[:, :, t], ta[t][:].indirect(idx[:]))
        inv_t = sb.tile([P, 2], F32, name="inv_t")
        nc.vector.reciprocal(inv_t[:], cols[:, 8:10])
        a_codes = sb.tile([P, I], U32, name="a_codes", align_bytes=64)
        a_sc = sb.tile([P, I], U8, name="a_sc", align_bytes=64)
        for h in range(2):
            nc.vector.tensor_copy(a_in[:, h * P : (h + 1) * P, 3], ta[3][:].indirect(idx[:, 8 * h : 8 * h + 8]))
        for h in range(2):
            hs = slice(h * P, (h + 1) * P)
            nc.vector.quantize_mx(out=a_codes[:, hs].bitcast(FP8X4), scales=a_sc[:, hs], in_=a_in[:, hs, :].rearrange("p i t -> p (i t)"))

        p_sb = [sb.tile([P, PACK, P], F32, name="p%d" % h, tag="p%d" % h, align_bytes=64) for h in range(2)]
        z0 = sb.tile([P, G], F32, name="z0")
        z1 = sb.tile([P, G], F32, name="z1", tag="late1", align_bytes=64)
        z = [z0, z1]
        for h in range(2):
            hs = slice(h * P, (h + 1) * P)
            s = bank(h, [P, J], "s%d" % h)
            nc.tensor.matmul_mx(out=s[:], lhsT=a_codes[:, hs].bitcast(FP8X4), lhsT_scale=a_sc[:, hs],
                                rhs=words_g[:].bitcast(FP4X4), rhs_scale=sc_g[:], start=True, stop=True)
            nc.scalar.activation(p_sb[h][:], s[:].rearrange("p (m t) -> p t m", t=PACK), ACT.Exp, scale=(cols[:, 8:9], t_last[:])[h])

        bg = {}
        bt_in = {}
        bt_codes = [sb.tile([P, P], U32, name="bt_codes%d" % c, align_bytes=64) for c in range(4)]
        bt_sc = [sb.tile([P, P], U8, name="bt_sc%d" % c, align_bytes=64) for c in range(4)]
        bt_ps = {}

        def gather_b(c):
            bg[c] = sb.tile([P, J], BF16, name="bg%d" % c, tag=("bg0", "p1", "bg2", "bg3")[c], align_bytes=64)
            nc.vector.tensor_copy(bg[c][:], br[c][:].indirect(idx2[:]))

        def turn_b(c):
            bt_ps[c] = bank(4 + c, [P, 2, P], "btp%d" % c)
            w = bg[c][:].bitcast(F32)
            for u in range(2):
                nc.tensor.transpose(bt_ps[c][:, u, :], w[:, u : J // 2 : 2], ident[:])

        def copy_b(c):
            bt_in[c] = sb.tile([P, P, PACK], BF16, name="bt_in%d" % c, tag="late%d" % (c + 2), align_bytes=64)
            nc.scalar.copy(bt_in[c][:].rearrange("p d t -> p (d t)").bitcast(F32).rearrange("p (d u) -> p d u", u=2),
                           bt_ps[c][:].rearrange("p u d -> p d u"))

        def quant_b(c):
            nc.vector.quantize_mx(out=bt_codes[c][:].bitcast(FP8X4), scales=bt_sc[c][:], in_=bt_in[c][:].rearrange("p d t -> p (d t)"))

        gather_b(0)
        for h in range(2):
            nc.vector.tensor_reduce(z[h][:], p_sb[h][:].rearrange("p t (g e) -> p g t e", e=2), AX.XY, ALU.add)
        lz = sb.tile([P, 2, G], F32, name="lz", tag="late0", align_bytes=64)
        for h in range(2):
            nc.scalar.activation(lz[:, h, :], z[h][:], ACT.Ln)
        inv_z = sb.tile([P, 2, G], F32, name="inv_z", tag="late2", align_bytes=64)
        nc.scalar.activation(inv_z[:], lz[:], ACT.Exp, scale=-1.0)
        th = sb.tile([P, 2, G], F32, name="th", tag="late1", align_bytes=64)
        for h in range(2):
            nc.scalar.activation(th[:, h, :], lz[:, h, :], ACT.Tanh, scale=inv_t[:, h : h + 1], bias=-2.0)
        sq = sb.tile([P, 2 * G], F32, name="sq", tag="late3", align_bytes=64)
        nc.scalar.activation(sq[:], th[:].rearrange("p h g -> p (h g)"), ACT.Square)

        pt = [bank(2 + b, [P, 2, I], "pt%d" % b) for b in range(2)]
        for t in range(PACK):
            for h in range(2):
                nc.tensor.transpose(pt[t // 2][:, t % 2, h * P : (h + 1) * P], p_sb[h][:, t, :], ident[:])
        turn_b(0)

        of = {0: ol[0]}
        nc.gpsimd.tensor_tensor(ol[0][:], ol[0][:], fade_bc[:], ALU.mult)
        for c in range(1, 4):
            gather_b(c)
        for c in range(1, 4):
            turn_b(c)

        pj = sb.tile([P, PACK, I], F32, name="pj", tag="late1", align_bytes=64)
        for t in range(PACK):
            nc.scalar.activation(pj[:, t, :], pt[t // 2][:, t % 2, :], ACT.Copy, scale=js_col[:, t : t + 1])

        ge = sb.tile([P, 2 * G], F32, name="ge", tag="late4", align_bytes=64)
        nc.vector.scalar_tensor_tensor(ge[:], inv_z[:].rearrange("p h g -> p (h g)"), -1.0, gw_sb[:].rearrange("p h g -> p (h g)"), ALU.mult, ALU.mult)
        rd = sb.tile([P, 2 * G, 2], F32, name="rd", tag="late5", align_bytes=64)
        nc.vector.scalar_tensor_tensor(rd[:], sq[:].unsqueeze(2).to_broadcast([P, 2 * G, 2]), 1.0,
                                       ge[:].unsqueeze(2).to_broadcast([P, 2 * G, 2]), ALU.subtract, ALU.mult)
        rt = bank(0, [P, I], "rt")
        for h in range(2):
            nc.tensor.transpose(rt[:, h * P : (h + 1) * P], rd[:, h * G : (h + 1) * G, :].rearrange("p g e -> p (g e)"), ident[:])
        for c in range(4):
            copy_b(c)
        g_in = sb.tile([P, I, PACK], BF16, name="g_in", tag="g_in", align_bytes=64)
        nc.vector.tensor_tensor(g_in[:], pj[:].rearrange("p t i -> p i t"), rt[:].unsqueeze(2).to_broadcast([P, I, PACK]), ALU.mult)
        quant_b(0)
        g_codes = sb.tile([P, I], U32, name="g_codes", align_bytes=64)
        g_sc = sb.tile([P, I], U8, name="g_sc", align_bytes=64)
        nc.vector.quantize_mx(out=g_codes[:].bitcast(FP8X4), scales=g_sc[:], in_=g_in[:].rearrange("p i t -> p (i t)"))
        for c in range(1, 4):
            quant_b(c)
        for c in range(4):
            if MODES[c] == "V":
                nc.vector.tensor_tensor(ol[c][:], ol[c][:], fade_bc[:], ALU.mult)

        of[1] = sb.tile([P, T], F32, name="of1", tag="late5", align_bytes=64)
        nc.gpsimd.tensor_tensor(of[1][:], ol[1][:], fade_bc[:], ALU.mult)
        gx_sb = [sb.tile([P, I], F32, name="gx%d" % c) for c in range(4)]
        for c in range(4):
            gx = bank((2, 3, 6, 7)[c], [P, I], "gxp%d" % c)
            nc.tensor.matmul_mx(out=gx[:], lhsT=bt_codes[c][:].bitcast(FP8X4), lhsT_scale=bt_sc[c][:],
                                rhs=g_codes[:].bitcast(FP8X4), rhs_scale=g_sc[:], start=True, stop=True)
            nc.scalar.copy(gx_sb[c][:], gx[:])

        back = {}
        oft = {}

        def fade_pair(c0):
            oft[c0] = sb.tile([P, 8, 2, P], F32, name="oft%d" % c0)
            for kk in range(4):
                ot = bank(2 + kk % 2, [P, 2, 2, P], "ot%d_%d" % (c0, kk))
                for e in range(2):
                    k = 2 * kk + e
                    for m in range(2):
                        nc.tensor.transpose(ot[:, e, m, :], ol[c0 + m][:, k * P : (k + 1) * P], ident[:])
                for e in range(2):
                    k = 2 * kk + e
                    nc.scalar.activation(oft[c0][:, k, :, :], ot[:, e, :, :], ACT.Copy, scale=cols[:, k : k + 1])

        def turn_back(c):
            for hf in range(2):
                back[(c, hf)] = bank((0, 1, 4, 5)[2 * (c % 2) + hf], [P, 4, P], "back%d_%d" % (c, hf))
                for e in range(4):
                    nc.tensor.transpose(back[(c, hf)][:, e, :], oft[c - c % 2][:, 4 * hf + e, c % 2, :], ident[:])

        for c0 in (0, 2):
            if MODES[c0] in ("X", "W"):
                fade_pair(c0)
        faded = {}
        for c in range(4):
            if MODES[c] in ("X", "W"):
                turn_back(c)
            if MODES[c] == "W":
                for hf in range(1):
                    faded[(c, hf)] = sb.tile([P, 512], F32, name="faded%d_%d" % (c, hf))
                    nc.scalar.copy(faded[(c, hf)][:], back[(c, hf)][:].rearrange("p e n -> p (e n)"))

        for c in range(4):
            nc.vector.tensor_copy(win[c][:].indirect(idx[:]), gx_sb[c][:])
            rows_c = slice(c * P, (c + 1) * P)
            if MODES[c] == "G":
                full = sb.tile([P, T], F32, name="full%d" % c, tag="full%d" % c, align_bytes=64)
                nc.gpsimd.tensor_tensor(full[:], of[c][:], win[c][:], ALU.add)
                nc.sync.dma_start(out[rows_c, :], full[:])
            else:
                for hf in range(2):
                    cs = slice(hf * 512, (hf + 1) * 512)
                    res = sb.tile([P, 512], F32, name="res%d_%d" % (c, hf))
                    if (c, hf) not in faded:
                        nc.vector.tensor_tensor(res[:], back[(c, hf)][:].rearrange("p e n -> p (e n)"), win[c][:, cs], ALU.add)
                    else:
                        nc.gpsimd.tensor_tensor(res[:], faded[(c, hf)][:], win[c][:, cs], ALU.add)
                    nc.sync.dma_start(out[rows_c, cs], res[:])
